import numpy as np
import ml_dtypes


def mxq(x, axis, fmt="e4m3"):
    dtype, down = {"e4m3": (ml_dtypes.float8_e4m3fn, 7), "e5m2": (ml_dtypes.float8_e5m2, 14)}[fmt]
    v = np.moveaxis(np.asarray(x, np.float32).astype(ml_dtypes.bfloat16).astype(np.float64), axis, -1)
    blocks = v.reshape(v.shape[:-1] + (-1, 32))
    amax = np.abs(blocks).max(-1, keepdims=True)
    byte = np.maximum(np.where(amax > 0, np.frexp(amax)[1] - 1 + 127, 0) - down, 1)
    scale = np.exp2(byte - 127.0)
    codes = (blocks / scale).astype(np.float32).astype(dtype).astype(np.float64)
    return np.moveaxis((codes * scale).reshape(v.shape), -1, axis)


WIDE = False


def mx_kscale(k):
    if not WIDE:
        return np.ones(k)
    levels = np.array([10, -10, 5, -5, 0])
    if k % 512:
        return np.exp2(np.random.permutation(np.resize(levels, k // 32))).repeat(32)
    a = np.empty((k // 512, 16))
    for p in range(k // 512):
        a[p, :8] = np.random.permutation(np.resize(levels, 8))
        for g in range(8):
            far = levels[np.abs(levels - a[p, g]) >= 10]
            a[p, g + 8] = far[np.random.randint(len(far))]
    return np.exp2(a.ravel()).repeat(32)


BF16 = ml_dtypes.bfloat16


def bf(x):
    return np.asarray(x, np.float32).astype(BF16)


def f64(x):
    return np.asarray(x).astype(np.float64)

E4M3FN = np.array([(-1.0 if i & 128 else 1.0) * ((1.0 + (i & 7) / 8.0) * 2.0 ** (((i >> 3) & 15) - 7) if i & 120 else (i & 7) * 2.0 ** -9) for i in range(256)])


def e4m3fn_bytes(y):
    return np.clip(np.asarray(y, np.float64), -448.0, 448.0).astype(np.float32).astype(ml_dtypes.float8_e4m3fn).view(np.uint8)


def e4m3fn_values(b):
    return E4M3FN[b]


L, D, T, E = 512, 1024, 3072, 1536


def setup_inputs():
    s, t = mx_kscale(D), mx_kscale(T)
    K = np.random.standard_normal((D, T)) * s[:, None]
    V = np.random.standard_normal((T, E)) / t[:, None]
    K_scale = (np.abs(K).max(axis=1, keepdims=True) / 448).astype(np.float32)
    V_scale = (np.abs(V).max(axis=1, keepdims=True) / 448).astype(np.float32)
    return {"Q": bf(np.random.standard_normal((L, D)) / s),
            "K_bytes": e4m3fn_bytes(K / f64(K_scale)),
            "K_scale": K_scale,
            "V_bytes": e4m3fn_bytes(V / f64(V_scale)),
            "V_scale": V_scale,
            "g": bf((1 + 0.1 * np.random.standard_normal(T)) / np.sqrt(T) * t)}


def reference(Q, K_bytes, K_scale, V_bytes, V_scale, g):
    K = e4m3fn_values(K_bytes) * np.repeat(f64(K_scale), T, axis=1)
    V = e4m3fn_values(V_bytes) * np.repeat(f64(V_scale), E, axis=1)
    S = mxq(f64(Q), 1, "e4m3") @ mxq(K, 0, "e4m3")
    x = S / np.sqrt(D)
    A = f64(g)[None, :] / (1 + np.exp(-x))
    return mxq(A, 1, "e4m3") @ mxq(V, 0, "e4m3")

from contextlib import ExitStack

import concourse.mybir as mybir
from concourse.masks import make_identity

L, D, T, E = 512, 1024, 3072, 1536
FLOPS = 2 * L * D * T + 2 * L * T * E

F32 = mybir.dt.float32
BF16 = mybir.dt.bfloat16
U32 = mybir.dt.uint32
U8 = mybir.dt.uint8
FP8 = mybir.dt.float8_e4m3fn
FP8X4 = mybir.dt.float8_e4m3fn_x4
MULT = mybir.AluOpType.mult
SIGMOID = mybir.ActivationFunctionType.Sigmoid

P = 128
PACK = 4
GROUP = P * PACK
N_PASS = D // GROUP
N_GROUP = T // GROUP
N_SWEEP = E // GROUP
N_LT = L // P


def tile_latent_sigmoid_read_d5_kernel(tc, Q, K_bytes, K_scale, V_bytes, V_scale, g, out):
    nc = tc.nc
    with ExitStack() as ctx:
        keep = ctx.enter_context(tc.tile_pool(name="keep", bufs=1))
        raw = ctx.enter_context(tc.tile_pool(name="raw", bufs=1))
        work = ctx.enter_context(tc.tile_pool(name="work", bufs=3))
        psum = ctx.enter_context(tc.psum_pool(name="psum", bufs=4))
        ctx.enter_context(tc.manual_schedule())

        ksc = keep.tile([P, N_PASS * PACK], F32, name="ksc")
        vsc = keep.tile([P, N_GROUP * PACK], F32, name="vsc")
        gb = keep.tile([P, N_GROUP * PACK], BF16, name="gb")
        g32 = keep.tile([P, N_GROUP * PACK], F32, name="g32")
        ident = keep.tile([P, P], F32, name="ident")
        k_view = K_bytes.rearrange("(c p j) n -> c p j n", p=P, j=PACK)
        v_view = V_bytes.rearrange("(g p t) e -> g p t e", p=P, t=PACK)
        k_at = {}
        v_at = {}
        q_raw = []

        def load_k(lo, hi):
            for c in range(N_PASS):
                kb = raw.tile([P, PACK, hi - lo], U8, name="kb_%d_%d" % (c, lo), align_bytes=64)
                nc.sync.dma_start(out=kb[:], in_=k_view[c, :, :, lo:hi])
                for x in range(lo // GROUP, hi // GROUP):
                    k_at[(x, c)] = (kb, x * GROUP - lo)

        def load_v(gi, lo, hi):
            vb = raw.tile([P, PACK, hi - lo], U8, name="vb_%d_%d" % (gi, lo), align_bytes=64)
            nc.sync.dma_start(out=vb[:], in_=v_view[gi, :, :, lo:hi])
            for e in range(lo // GROUP, hi // GROUP):
                v_at[(gi, e)] = (vb, e * GROUP - lo)

        nc.sync.dma_start(out=ksc[:].rearrange("p (c j) -> p c j", j=PACK), in_=K_scale.rearrange("(c p j) o -> p c (j o)", p=P, j=PACK))
        load_k(0, GROUP)
        for lt in range(N_LT):
            qr = raw.tile([P, D], BF16, name="q_raw_%d" % lt, align_bytes=64)
            nc.sync.dma_start(out=qr[:], in_=Q[lt * P : (lt + 1) * P, :])
            q_raw.append(qr)
        nc.sync.dma_start(out=vsc[:].rearrange("p (c j) -> p c j", j=PACK), in_=V_scale.rearrange("(c p j) o -> p c (j o)", p=P, j=PACK))
        nc.sync.dma_start(out=gb[:].rearrange("p (c j) -> p c j", j=PACK), in_=g.rearrange("(c p j) -> p c j", p=P, j=PACK))
        load_v(0, 0, GROUP)
        load_k(GROUP, 3 * GROUP)
        load_v(1, 0, GROUP)
        load_v(2, 0, GROUP)
        load_k(3 * GROUP, 6 * GROUP)
        for gi in range(3, N_GROUP):
            load_v(gi, 0, GROUP)
        for gi in range(N_GROUP):
            load_v(gi, GROUP, E)

        make_identity(nc, ident[:])

        chunks = []
        for gi in range(N_GROUP):
            chunks.append(("k", gi, 0))
            chunks.append(("k", gi, 1))
            chunks.append(("v", gi, 0))
        for e in range(1, N_SWEEP):
            for gi in range(N_GROUP):
                chunks.append(("v", gi, e))
        planes = {}
        grouped = {}
        codes = {}

        def paired(i):
            return i >= 3 * N_GROUP and i % 3 == 2

        def widen(i):
            kind, gi, x = chunks[i]
            if kind == "k":
                tile, off = k_at[(gi, x)]
                sc, s0 = ksc, x * PACK
            else:
                tile, off = v_at[(gi, x)]
                sc, s0 = vsc, gi * PACK
            pl = work.tile([P, PACK * GROUP], BF16, name="pl", tag="pl", align_bytes=64)
            for t in range(PACK):
                if paired(i):
                    dst = pl[:].rearrange("p (u n e) -> p u n e", u=2, e=2)[:, t // 2, :, t % 2]
                else:
                    dst = pl[:, t * GROUP : (t + 1) * GROUP]
                nc.vector.tensor_scalar(out=dst, in0=tile[:, t, off : off + GROUP].bitcast(FP8), scalar1=sc[:, s0 + t : s0 + t + 1], scalar2=None, op0=MULT)
            planes[i] = pl

        def interleave(i):
            kind, gi, x = chunks[i]
            pl = planes.pop(i)
            gr = work.tile([P, PACK * GROUP], BF16, name="gr", tag="gr", align_bytes=64)
            if kind == "k":
                src = pl[:].rearrange("p (j mo mi t) -> p t mo j mi", j=PACK, mi=2, t=PACK)
                dst = gr[:].rearrange("p (t mo mi j) -> p t mo j mi", t=PACK, mi=2, j=PACK)
                for t in range(PACK):
                    if x == 1 and t == 3:
                        nc.vector.tensor_copy(out=dst[:, t], in_=src[:, t])
                    else:
                        nc.scalar.copy(out=dst[:, t], in_=src[:, t])
            elif paired(i):
                src = pl[:].bitcast(F32).rearrange("p (u no ni) -> p no u ni", u=2, ni=4)
                dst = gr[:].bitcast(F32).rearrange("p (no ni u) -> p no u ni", ni=4, u=2)
                nc.scalar.copy(out=dst, in_=src)
            else:
                src = pl[:].rearrange("p (t no ni) -> p no t ni", t=PACK, ni=4)
                dst = gr[:].rearrange("p (no ni t) -> p no t ni", ni=4, t=PACK)
                nc.scalar.copy(out=dst, in_=src)
            grouped[i] = gr

        def quantize_tile(src, cd, cs):
            nc.vector.quantize_mx(out=cd.bitcast(FP8X4), scales=cs, in_=src)

        def quantize(i):
            cd = work.tile([P, GROUP], U32, name="cd", tag="cd", bufs=4, align_bytes=64)
            cs = work.tile([P, GROUP], U8, name="cs", tag="cs", bufs=4, align_bytes=64)
            quantize_tile(grouped.pop(i)[:], cd[:], cs[:])
            codes[i] = (cd, cs)

        qc = []
        qs = []

        def prepare_q():
            q_grouped = []
            for c in range(N_PASS):
                qg = keep.tile([P, PACK * L], BF16, name="qg_%d" % c, align_bytes=64)
                q_grouped.append(qg)
                for h in range(2):
                    xt = psum.tile([P, 2, 2, P], F32, name="xt", tag="o")
                    for a in range(2):
                        words = q_raw[2 * h + a][:].bitcast(F32)
                        for u in range(2):
                            nc.tensor.transpose(xt[:, a, u, :], words[:, 256 * c + u : 256 * (c + 1) : 2], ident[:])
                    nc.vector.tensor_copy(
                        out=qg[:].bitcast(F32).rearrange("p (h a r u) -> p h a r u", h=2, a=2, u=2)[:, h],
                        in_=xt[:].rearrange("p a u r -> p a r u"),
                    )
            for c in range(N_PASS):
                cd = keep.tile([P, L], U32, name="qc_%d" % c, align_bytes=64)
                cs = keep.tile([P, L], U8, name="qs_%d" % c, align_bytes=64)
                quantize_tile(q_grouped[c][:], cd[:], cs[:])
                qc.append(cd)
                qs.append(cs)

        s_banks = {}
        sig = {}
        a_grouped = {}
        ac = {}

        def scores(gi):
            banks = []
            for t in range(PACK):
                sb = psum.tile([P, L], F32, name="sb", tag="s")
                for c in range(N_PASS):
                    cd, cs = codes[3 * gi + c]
                    cols = slice(t * P, (t + 1) * P)
                    nc.tensor.matmul_mx(
                        out=sb[:], lhsT=cd[:, cols].bitcast(FP8X4), lhsT_scale=cs[:, cols],
                        rhs=qc[c][:].bitcast(FP8X4), rhs_scale=qs[c][:], start=(c == 0), stop=(c == N_PASS - 1),
                    )
                banks.append(sb)
            s_banks[gi] = banks

        def sigma(gi):
            sg = work.tile([P, PACK * L], F32, name="sg", tag="sg", bufs=2, align_bytes=64)
            for t in range(PACK):
                nc.scalar.activation(out=sg[:, t * L : (t + 1) * L], in_=s_banks[gi][t][:], func=SIGMOID, scale=1.0 / 32.0)
            sig[gi] = sg

        def gain(gi):
            ag = work.tile([P, PACK * L], BF16, name="ag", tag="ag", bufs=2, align_bytes=64)
            gcol = g32[:, PACK * gi : PACK * (gi + 1)].rearrange("p (o t i) -> p o t i", o=1, i=1)
            nc.vector.tensor_tensor(
                out=ag[:].rearrange("p (no ni t) -> p no t ni", ni=4, t=PACK),
                in0=sig[gi][:].rearrange("p (t no ni) -> p no t ni", t=PACK, ni=4),
                in1=gcol.to_broadcast([P, L // 4, PACK, 4]),
                op=MULT,
            )
            a_grouped[gi] = ag

        def quantize_a(gi):
            cd = keep.tile([P, L], U32, name="ac_%d" % gi, align_bytes=64)
            cs = keep.tile([P, L], U8, name="as_%d" % gi, align_bytes=64)
            quantize_tile(a_grouped[gi][:], cd[:], cs[:])
            ac[gi] = (cd, cs)

        acc = {}

        def mix(i):
            kind, gi, e = chunks[i]
            vd, vs = codes[i]
            cd, cs = ac[gi]
            for lt in range(N_LT):
                if gi == 0:
                    ob = psum.tile([P, GROUP], F32, name="ob", tag="s" if e == 1 else "o")
                    acc[(e, lt)] = ob
                cols = slice(lt * P, (lt + 1) * P)
                nc.tensor.matmul_mx(
                    out=acc[(e, lt)][:], lhsT=cd[:, cols].bitcast(FP8X4), lhsT_scale=cs[:, cols],
                    rhs=vd[:].bitcast(FP8X4), rhs_scale=vs[:], start=(gi == 0), stop=(gi == N_GROUP - 1),
                )

        def finish(e, lt):
            res = work.tile([P, GROUP], F32, name="res", tag="res", bufs=4, align_bytes=64)
            if lt % 2 == 0:
                nc.vector.tensor_copy(out=res[:], in_=acc[(e, lt)][:])
            else:
                nc.scalar.copy(out=res[:], in_=acc[(e, lt)][:])
            nc.sync.dma_start(out=out[lt * P : (lt + 1) * P, e * GROUP : (e + 1) * GROUP], in_=res[:])

        n = len(chunks)
        first_v2 = 3 * N_GROUP
        for s in range(-3, n):
            a_step = s - 4
            if s >= 0 and s % 3 == 2 and s // 3 < N_GROUP:
                sigma(s // 3)
            if a_step >= 0 and a_step % 3 == 0 and a_step // 3 < N_GROUP:
                quantize_a(a_step // 3)
                mix(3 * (a_step // 3) + 2)
            if s == -1:
                prepare_q()
            if s + 3 < n:
                widen(s + 3)
            if s == -1:
                nc.vector.tensor_copy(out=g32[:], in_=gb[:])
            if 0 <= s + 2 < n:
                interleave(s + 2)
            if s >= 3 and s % 3 == 0 and s // 3 - 1 < N_GROUP:
                gain(s // 3 - 1)
            for e in range(N_SWEEP - 1):
                base = first_v2 + 2 + N_GROUP * e
                if s in (base, base + 1):
                    finish(e, 2 * (s - base))
                    finish(e, 2 * (s - base) + 1)
            if s >= 0:
                quantize(s)
                if s >= first_v2:
                    mix(s)
                elif s % 3 == 1:
                    scores(s // 3)
        for lt in range(N_LT):
            finish(N_SWEEP - 1, lt)
